import numpy as np
import ml_dtypes


def mxq(x, axis, fmt="e4m3"):
    dtype, down = {"e4m3": (ml_dtypes.float8_e4m3fn, 7), "e5m2": (ml_dtypes.float8_e5m2, 14)}[fmt]
    v = np.moveaxis(np.asarray(x, np.float32).astype(ml_dtypes.bfloat16).astype(np.float64), axis, -1)
    blocks = v.reshape(v.shape[:-1] + (-1, 32))
    amax = np.abs(blocks).max(-1, keepdims=True)
    byte = np.maximum(np.where(amax > 0, np.frexp(amax)[1] - 1 + 127, 0) - down, 1)
    scale = np.exp2(byte - 127.0)
    codes = (blocks / scale).astype(np.float32).astype(dtype).astype(np.float64)
    return np.moveaxis((codes * scale).reshape(v.shape), -1, axis)


WIDE = False


def mx_kscale(k):
    if not WIDE:
        return np.ones(k)
    levels = np.array([30, -30])
    if k % 512:
        return np.exp2(np.random.permutation(np.resize(levels, k // 32))).repeat(32)
    a = np.empty((k // 512, 16))
    for p in range(k // 512):
        a[p, :8] = np.random.permutation(np.resize(levels, 8))
        for g in range(8):
            far = levels[np.abs(levels - a[p, g]) >= 10]
            a[p, g + 8] = far[np.random.randint(len(far))]
    return np.exp2(a.ravel()).repeat(32)


BF16 = ml_dtypes.bfloat16


def bf(x):
    return np.asarray(x, np.float32).astype(BF16)


def f64(x):
    return np.asarray(x).astype(np.float64)


E2M1 = np.array([0.0, 0.5, 1.0, 1.5, 2.0, 3.0, 4.0, 6.0, -0.0, -0.5, -1.0, -1.5, -2.0, -3.0, -4.0, -6.0])


def pack_weight(w, fmt):
    k, n = w.shape
    w = f64(bf(w)).reshape(k // 32, 32, n)
    amax = np.abs(w).max(1)
    if fmt == "e4m3":
        byte = np.frexp(amax)[1] - 1 + 127 - 7
    else:
        mant, ex = np.frexp(amax / 6.0)
        byte = np.where(mant > 0.5, ex, ex - 1) + 127
    byte = np.clip(np.where(amax > 0, byte, 1), 1, 254)
    scaled = (w * np.exp2(127.0 - byte)[:, None, :]).reshape(k, n).astype(np.float32)
    by_word = np.ascontiguousarray(scaled.reshape(k // 512, 128, 4, n).transpose(0, 1, 3, 2))
    if fmt == "e4m3":
        words = by_word.astype(ml_dtypes.float8_e4m3fn).view(np.uint8)
    else:
        c = by_word.astype(ml_dtypes.float4_e2m1fn).view(np.uint8) & 0xF
        words = c[..., 0::2] | (c[..., 1::2] << 4)
    return np.ascontiguousarray(words), np.ascontiguousarray(byte.astype(np.uint8).reshape(k // 512, 16, n))


def unpack_weight(words, scales, fmt):
    g, p, n, _ = words.shape
    if fmt == "e4m3":
        vals = np.ascontiguousarray(words).view(ml_dtypes.float8_e4m3fn).astype(np.float64)
    else:
        nib = np.empty((g, p, n, 4), np.uint8)
        nib[..., 0::2] = words & 0xF
        nib[..., 1::2] = words >> 4
        vals = E2M1[nib]
    vals = vals * np.repeat(np.exp2(scales.astype(np.float64) - 127.0), 8, axis=1)[..., None]
    return vals.transpose(0, 1, 3, 2).reshape(g * 512, n)
def pack4(w):
    words, scales = pack_weight(w, "e2m1")
    return words.reshape(words.shape[0], 128, -1), scales


def unpack4(words, scales):
    return unpack_weight(words.reshape(words.shape[0], 128, -1, 2), scales, "e2m1")


B, M, N = 1024, 2048, 1024

ALPHA = 1.6


def setup_inputs():
    s = mx_kscale(M)
    t = mx_kscale(N)
    z = bf(np.random.standard_normal((B, M)))
    y = bf(np.random.standard_normal((B, M)) * s)
    rho = bf(np.exp(0.3 * np.random.standard_normal(M)) * s)
    a_words, a_scales = pack4(np.random.standard_normal((M, N)) / np.sqrt(M) / s[:, None] * t)
    c = bf(np.random.standard_normal((B, N)) * t)
    kkt_inv = bf(np.random.standard_normal((N, N)) / np.sqrt(N) / t[:, None])
    x = bf(np.random.standard_normal((B, N)))
    return {"z": z, "y": y, "rho": rho, "a_words": a_words, "a_scales": a_scales,
            "c": c, "kkt_inv": kkt_inv, "x": x}


def reference(z, y, rho, a_words, a_scales, c, kkt_inv, x):
    v = f64(rho) * f64(z) - f64(y)
    atv = mxq(v, 1, "e4m3") @ unpack4(a_words, a_scales)
    r = atv - f64(c)
    sol = mxq(r, 1, "e5m2") @ mxq(f64(kkt_inv), 0, "e4m3")
    return ALPHA * sol + (1.0 - ALPHA) * f64(x)

@@ -1,0 +1,310 @@
+from contextlib import ExitStack
+
+import concourse.mybir as mybir
+from concourse.masks import make_identity
+
+F32 = mybir.dt.float32
+BF16 = mybir.dt.bfloat16
+I32 = mybir.dt.int32
+U32 = mybir.dt.uint32
+U8 = mybir.dt.uint8
+E4M3 = mybir.dt.float8_e4m3fn_x4
+E5M2 = mybir.dt.float8_e5m2_x4
+E2M1 = mybir.dt.float4_e2m1fn_x4
+COPY = mybir.ActivationFunctionType.Copy
+ADD = mybir.AluOpType.add
+MULT = mybir.AluOpType.mult
+SUB = mybir.AluOpType.subtract
+
+P = 128
+B, M, N = 1024, 2048, 1024
+TILES = B // P
+G1 = M // 512
+G2 = N // 512
+FLOPS = 2 * B * M * N + 2 * B * N * N
+
+
+def tile_admm_kkt_step_s9_kernel(tc, z, y, rho, a_words, a_scales, c, kkt_inv, x, out):
+    nc = tc.nc
+    with ExitStack() as ctx:
+        keep = ctx.enter_context(tc.tile_pool(name="keep", bufs=1))
+        work = ctx.enter_context(tc.tile_pool(name="work", bufs=3))
+        psum = ctx.enter_context(tc.psum_pool(name="psum", bufs=2))
+        ctx.enter_context(tc.manual_schedule())
+
+        ident = keep.tile([P, P], F32, name="ident")
+        rho_row = keep.tile([P, 512], BF16, name="rho_row")
+        rho_col = keep.tile([P, G1, 4], F32, name="rho_col")
+        a_sb = keep.tile([P, G1, 2 * N], U8, name="a_sb", align_bytes=64)
+        a_sc = keep.tile([P, G1, N], U8, name="a_sc", align_bytes=64)
+        k_codes = keep.tile([P, G2, N], U32, name="k_codes", align_bytes=64)
+        k_sc = keep.tile([P, G2, N], U8, name="k_sc", align_bytes=64)
+        k_raw = [keep.tile([P, 4, N], BF16, name="k_raw%d" % h) for h in range(G2)]
+        z_sb = [keep.tile([P, M], BF16, name="z%d" % i) for i in range(TILES)]
+        y_sb = [keep.tile([P, M], BF16, name="y%d" % i) for i in range(TILES)]
+        c_sb = [keep.tile([P, N], BF16, name="c%d" % i) for i in range(TILES)]
+        x_sb = [keep.tile([P, N], BF16, name="x%d" % i) for i in range(TILES)]
+
+        make_identity(nc, ident[:])
+        nc.vector.memset(rho_row[:], 0.0)
+        nc.vector.memset(a_sc[:].rearrange("p g n -> p (g n)").bitcast(I32), 0)
+
+        def rows(i):
+            return slice(i * P, (i + 1) * P)
+
+        def load_zy(i):
+            nc.sync.dma_start(out=z_sb[i][:], in_=z[rows(i), :])
+            nc.sync.dma_start(out=y_sb[i][:], in_=y[rows(i), :])
+
+        def load_c(i):
+            nc.sync.dma_start(out=c_sb[i][:], in_=c[rows(i), :])
+
+        def load_x(i):
+            nc.sync.dma_start(out=x_sb[i][:], in_=x[rows(i), :])
+
+        def load_k(h):
+            nc.sync.dma_start(
+                out=k_raw[h][:],
+                in_=kkt_inv[512 * h : 512 * (h + 1), :].rearrange("(p j) w -> p j w", j=4),
+            )
+
+        nc.sync.dma_start(out=rho_row[0:G1, :], in_=rho.rearrange("(g k) -> g k", g=G1))
+        for half in range(2):
+            cols = slice(half * 1024, (half + 1) * 1024)
+            nc.sync.dma_start(out=z_sb[0][:, cols], in_=z[rows(0), cols])
+            nc.sync.dma_start(out=y_sb[0][:, cols], in_=y[rows(0), cols])
+        load_zy(1)
+        for r in range(4):
+            nc.sync.dma_start(
+                out=a_sc[r:P:32].bitcast(I32),
+                in_=a_scales[:, r:16:4, :].rearrange("g q n -> q g n").bitcast(I32),
+            )
+        for g in range(G1):
+            nc.sync.dma_start(out=a_sb[:, g, :], in_=a_words[g])
+        load_c(0)
+        load_zy(2)
+        load_k(0)
+        load_zy(3)
+        load_c(1)
+        load_k(1)
+        load_c(2)
+        for i in range(4, TILES):
+            load_zy(i)
+            load_c(i - 1)
+            load_x(i - 4)
+        load_c(TILES - 1)
+        for i in range(TILES - 4, TILES):
+            load_x(i)
+
+        rho_t = psum.tile([P, 512], F32, name="acc2")
+        for u in range(2):
+            nc.tensor.transpose(
+                rho_t[:, u * P : (u + 1) * P], rho_row[:].bitcast(F32)[:, u:256:2], ident[:]
+            )
+        nc.vector.tensor_copy(
+            out=rho_col[:].rearrange("p g (u e) -> p g u e", e=2),
+            in_=rho_t[:, 0:256].bitcast(BF16).rearrange("p (u r e) -> p r u e", u=2, e=2)[:, 0:G1],
+        )
+
+        v_codes, v_sc = {}, {}
+        v_half, r_bf, x06, acc1, acc2, r_codes, r_sc = {}, {}, {}, {}, {}, {}, {}
+        zt, yt, zr = {}, {}, {}
+
+        def transpose_half(i, a):
+            zt[i, a] = psum.tile([P, 512], F32, name="zt")
+            yt[i, a] = psum.tile([P, 512], F32, name="yt")
+            for src, dst in ((z_sb[i], zt[i, a]), (y_sb[i], yt[i, a])):
+                words = src[:].bitcast(F32)
+                for gl in range(2):
+                    for u in range(2):
+                        base = 256 * (2 * a + gl)
+                        k = 2 * u + gl
+                        nc.tensor.transpose(
+                            dst[:, k * P : (k + 1) * P], words[:, base + u : base + 256 : 2], ident[:]
+                        )
+
+        def scale_half(i, a):
+            zr[i, a] = work.tile([P, 4, 2, P], F32, name="zr")
+            src = zt[i, a][:].bitcast(BF16).rearrange("p (u g b e) -> p g u e b", g=2, u=2, e=2)
+            for gl in range(2):
+                for t in range(4):
+                    nc.scalar.activation(
+                        out=zr[i, a][:, t, gl, :],
+                        in_=src[:, gl, t // 2, t % 2, :],
+                        func=COPY,
+                        scale=rho_col[:, 2 * a + gl, t : t + 1],
+                    )
+
+        def sub_half(i, a):
+            v_half[i, a] = work.tile([P, 2, P * 4], BF16, name="v_half", bufs=4, align_bytes=64)
+            nc.vector.tensor_tensor(
+                out=v_half[i, a][:].rearrange("p g (b u e) -> p (g b) u e", u=2, e=2),
+                in0=zr[i, a][:].rearrange("p (u e) g b -> p (g b) u e", e=2),
+                in1=yt[i, a][:].bitcast(BF16).rearrange("p (u q e) -> p q u e", u=2, e=2),
+                op=SUB,
+            )
+
+        def quant_v(i, a):
+            if a == 0:
+                v_codes[i] = work.tile([P, G1, P], U32, name="v_codes", align_bytes=64)
+                v_sc[i] = work.tile([P, G1, P], U8, name="v_sc", align_bytes=64)
+            gs = slice(2 * a, 2 * a + 2)
+            nc.vector.quantize_mx(
+                out=v_codes[i][:, gs, :].rearrange("p g b -> p (g b)").bitcast(E4M3),
+                scales=v_sc[i][:, gs, :].rearrange("p g b -> p (g b)"),
+                in_=v_half[i, a][:].rearrange("p g q -> p (g q)"),
+            )
+
+        def mm1(i, h):
+            acc1[i, h] = psum.tile([P, 512], F32, name="acc1")
+            for g in range(G1):
+                nc.tensor.matmul_mx(
+                    out=acc1[i, h][:],
+                    lhsT=v_codes[i][:, g, :].bitcast(E4M3),
+                    lhsT_scale=v_sc[i][:, g, :],
+                    rhs=a_sb[:, g, 1024 * h : 1024 * (h + 1)].bitcast(E2M1),
+                    rhs_scale=a_sc[:, g, 512 * h : 512 * (h + 1)],
+                    start=(g == 0),
+                    stop=(g == G1 - 1),
+                )
+
+        def residual(i, h):
+            if h == 0:
+                r_bf[i] = work.tile([P, N], BF16, name="r_bf", bufs=5, align_bytes=64)
+            cols = slice(512 * h, 512 * (h + 1))
+            nc.vector.tensor_tensor(
+                out=r_bf[i][:, cols].rearrange("p (u q e) -> p u q e", u=2, e=2),
+                in0=acc1[i, h][:].rearrange("p (q u e) -> p u q e", u=2, e=2),
+                in1=c_sb[i][:, cols].rearrange("p (q u e) -> p u q e", u=2, e=2),
+                op=SUB,
+            )
+
+        r_t, r_il = {}, {}
+
+        def transpose_r(i):
+            r_t[i] = psum.tile([P, 512], F32, name="zt" if i >= 5 else "acc2")
+            words = r_bf[i][:].bitcast(F32)
+            for k in range(4):
+                nc.tensor.transpose(
+                    r_t[i][:, k * P : (k + 1) * P], words[:, k * P : (k + 1) * P], ident[:]
+                )
+
+        def copy_r(i):
+            r_il[i] = work.tile([P, 512, 2], BF16, name="r_il", bufs=2, align_bytes=64)
+            nc.scalar.copy(
+                out=r_il[i][:].rearrange("p q e -> p (q e)").bitcast(F32).rearrange("p (h b u) -> p h b u", h=2, u=2),
+                in_=r_t[i][:].rearrange("p (h u b) -> p h b u", h=2, u=2),
+            )
+
+        def quant_r(i):
+            r_codes[i] = work.tile([P, G2 * P], U32, name="r_codes", bufs=4, align_bytes=64)
+            r_sc[i] = work.tile([P, G2 * P], U8, name="r_sc", bufs=4, align_bytes=64)
+            nc.vector.quantize_mx(
+                out=r_codes[i][:].bitcast(E5M2),
+                scales=r_sc[i][:],
+                in_=r_il[i][:].rearrange("p q e -> p (q e)"),
+            )
+
+        def mm2(i):
+            for n in range(2):
+                acc2[i, n] = psum.tile([P, 512], F32, name="yt" if i == 6 else "acc2")
+                for h in range(G2):
+                    nc.tensor.matmul_mx(
+                        out=acc2[i, n][:],
+                        lhsT=r_codes[i][:, h * P : (h + 1) * P].bitcast(E5M2),
+                        lhsT_scale=r_sc[i][:, h * P : (h + 1) * P],
+                        rhs=k_codes[:, h, 512 * n : 512 * (n + 1)].bitcast(E4M3),
+                        rhs_scale=k_sc[:, h, 512 * n : 512 * (n + 1)],
+                        start=(h == 0),
+                        stop=(h == G2 - 1),
+                    )
+
+        def scale_x(i):
+            x06[i] = work.tile([P, N], F32, name="x06", bufs=3)
+            nc.scalar.activation(out=x06[i][:], in_=x_sb[i][:], func=COPY, scale=-0.6)
+
+        def finish(i):
+            for n in range(2):
+                cols = slice(512 * n, 512 * (n + 1))
+                o = work.tile([P, 512], F32, name="o", bufs=6)
+                nc.vector.scalar_tensor_tensor(
+                    out=o[:], in0=acc2[i, n][:], scalar=1.6, in1=x06[i][:, cols], op0=MULT, op1=ADD
+                )
+                nc.sync.dma_start(out=out[rows(i), cols], in_=o[:])
+
+        k_il = {}
+
+        def inter_k(h, n, part):
+            if part == 0:
+                k_il[h, n] = work.tile([P, 512, 4], BF16, name="k_il", bufs=4, align_bytes=64)
+            w0 = 256 * part
+            dst = k_il[h, n][:, w0 : w0 + 256, :].rearrange("p (c i) t -> p c t i", i=4)
+            src = k_raw[h][:, :, 512 * n + w0 : 512 * n + w0 + 256].rearrange("p t (c i) -> p c t i", i=4)
+            nc.gpsimd.tensor_scalar(out=dst, in0=src, scalar1=1.0, scalar2=0.0, op0=MULT, op1=ADD)
+
+        def quant_k(h, n):
+            cols = slice(512 * n, 512 * (n + 1))
+            nc.vector.quantize_mx(
+                out=k_codes[:, h, cols].bitcast(E4M3),
+                scales=k_sc[:, h, cols],
+                in_=k_il[h, n][:].rearrange("p w t -> p (w t)"),
+            )
+
+        for a in range(2):
+            transpose_half(0, a)
+            scale_half(0, a)
+        for a in range(2):
+            sub_half(0, a)
+        for a in range(2):
+            quant_v(0, a)
+
+        for s in range(TILES):
+            nxt = s + 1
+            if s >= 5:
+                finish(1 if s == 5 else s - 4)
+            if nxt < TILES:
+                for a in range(2):
+                    transpose_half(nxt, a)
+                    scale_half(nxt, a)
+                    sub_half(nxt, a)
+            for j in [0, 1] if s == 3 else [s - 2] if s >= 4 else []:
+                transpose_r(j)
+                copy_r(j)
+                quant_r(j)
+            if s == 4:
+                mm2(0)
+                finish(0)
+            mm1(s, 0)
+            mm1(s, 1)
+            residual(s, 0)
+            if nxt < TILES:
+                quant_v(nxt, 0)
+            residual(s, 1)
+            if nxt < TILES:
+                quant_v(nxt, 1)
+            if s == 1:
+                for h in range(2):
+                    for n in range(2):
+                        for part in range(2):
+                            inter_k(h, n, part)
+            if s == 2:
+                quant_k(0, 0)
+            if s == 3:
+                quant_k(0, 1)
+                quant_k(1, 0)
+                quant_k(1, 1)
+                scale_x(0)
+                scale_x(1)
+            if s >= 4:
+                mm2(1 if s == 4 else s - 3)
+                scale_x(s - 2)
+        finish(4)
+        for j in (6, 7):
+            transpose_r(j)
+            copy_r(j)
+            quant_r(j)
+            mm2(j - 1)
+            scale_x(j)
+            finish(j - 1)
+        mm2(7)
+        finish(7)

@@ -30,7 +30,6 @@ def tile_admm_kkt_step_s9_kernel(tc, z, y, rho, a_words, a_scales, c, kkt_inv, x
         keep = ctx.enter_context(tc.tile_pool(name="keep", bufs=1))
         work = ctx.enter_context(tc.tile_pool(name="work", bufs=3))
         psum = ctx.enter_context(tc.psum_pool(name="psum", bufs=2))
-        ctx.enter_context(tc.manual_schedule())
 
         ident = keep.tile([P, P], F32, name="ident")
         rho_row = keep.tile([P, 512], BF16, name="rho_row")
@@ -240,7 +239,14 @@ def tile_admm_kkt_step_s9_kernel(tc, z, y, rho, a_words, a_scales, c, kkt_inv, x
             w0 = 256 * part
             dst = k_il[h, n][:, w0 : w0 + 256, :].rearrange("p (c i) t -> p c t i", i=4)
             src = k_raw[h][:, :, 512 * n + w0 : 512 * n + w0 + 256].rearrange("p t (c i) -> p c t i", i=4)
-            nc.gpsimd.tensor_scalar(out=dst, in0=src, scalar1=1.0, scalar2=0.0, op0=MULT, op1=ADD)
+            if (h + n) % 2 == 0:
+                nc.scalar.copy(out=dst, in_=src)
+            else:
+                nc.gpsimd.tensor_scalar(
+                    out=k_il[h, n][:, w0 : w0 + 256, :],
+                    in0=k_raw[h][:, :, 512 * n + w0 : 512 * n + w0 + 256].rearrange("p t w -> p w t"),
+                    scalar1=1.0, scalar2=0.0, op0=MULT, op1=ADD,
+                )
 
         def quant_k(h, n):
             cols = slice(512 * n, 512 * (n + 1))
@@ -282,11 +288,10 @@ def tile_admm_kkt_step_s9_kernel(tc, z, y, rho, a_words, a_scales, c, kkt_inv, x
             residual(s, 1)
             if nxt < TILES:
                 quant_v(nxt, 1)
-            if s == 1:
-                for h in range(2):
-                    for n in range(2):
-                        for part in range(2):
-                            inter_k(h, n, part)
+            if s == 1 or s == 2:
+                for n in range(2):
+                    for part in range(2):
+                        inter_k(s - 1, n, part)
             if s == 2:
                 quant_k(0, 0)
             if s == 3:

@@ -18,10 +18,27 @@ SUB = mybir.AluOpType.subtract
 
 P = 128
 B, M, N = 1024, 2048, 1024
+PAIRS = B // (2 * P)
 TILES = B // P
 G1 = M // 512
 G2 = N // 512
 FLOPS = 2 * B * M * N + 2 * B * N * N
+LOADS = "Z00 Z01 Z10 Z11 A c0 c1 k0 c2 k1 Z20 Z21 c3 x0 x1 c4 c5 Z30 Z31 x2 x3 c6 c7 x4 x5 x6 x7"
+ORDER = (
+    "Tz00 Tz01 zr000 zr001 Ty00 zr002 zr003 Ty01 zr010 v00 zr011 Tz02 zr012 zr013 zr020 Ty02 qv00 "
+    "zr021 v01 zr022 Tz03 zr023 zr030 Tz10 v02 zr031 Ty03 zr032 zr033 zr100 qv01 Ty10 zr101 qv02 "
+    "zr102 Tz11 v03 zr103 Tz12 zr110 zr111 v10 Ty11 zr112 zr113 zr120 Tz13 qv03 zr121 qv10 zr122 Ty12 "
+    "zr123 v11 zr130 zr131 zr132 M1_0 v12 zr133 qv11 Ty13 qv12 M1_1 r0 v13 M1_2 ik000S r1 qv13 M1_3 "
+    "r2 ik001S M1_4 r3 ik010S qk00 ik100G M1_5 r4 ik011S ik101G Tz20 r5 Tz21 zr200 qk01 Ty20 zr201 "
+    "ik110G zr202 Ty21 qk10 zr203 rT0 zr210 v20 Tz22 ik111G rc0 M1_6 zr211 qr0 zr212 qv20 zr213 qk11 "
+    "zr220 Ty22 zr221 v21 zr222 M2_00 zr223 x06_0 M2_01 v22 Tz23 x06_1 Ty23 qv21 qv22 Tz30 o00 zr230 "
+    "M1_7 zr231 o01 zr232 zr233 r6 zr300 Ty30 zr301 v23 zr302 Tz31 zr303 rT1 zr310 Tz32 v30 rc1 Ty31 "
+    "zr311 rT2 zr312 qv23 Ty32 qv30 rc2 qr1 M1_8 zr313 r7 zr320 zr321 qr2 M2_10 zr322 v31 zr323 M2_11 "
+    "x06_2 o10 Tz33 Ty33 qv31 zr330 o11 zr331 M2_20 zr332 r8 zr333 M2_21 x06_3 v32 M1_9 x06_4 o20 "
+    "M1_10 qv32 r9 rT3 o21 M1_11 rc3 v33 x06_5 rT4 qr3 rc4 qv33 M2_30 r10 M2_31 r11 M1_12 qr4 o30 "
+    "M1_13 o31 r12 x06_6 M2_40 r13 M2_41 o40 M1_14 o41 M1_15 x06_7 r14 rT5 r15 rT6 rc5 rc6 rT7 qr5 "
+    "rc7 M2_50 qr6 M2_51 o50 o51 M2_60 qr7 M2_61 o60 o61 M2_70 M2_71 o70 o71 "
+)
 
 
 def tile_admm_kkt_step_s9_kernel(tc, z, y, rho, a_words, a_scales, c, kkt_inv, x, out):
@@ -30,6 +47,7 @@ def tile_admm_kkt_step_s9_kernel(tc, z, y, rho, a_words, a_scales, c, kkt_inv, x
         keep = ctx.enter_context(tc.tile_pool(name="keep", bufs=1))
         work = ctx.enter_context(tc.tile_pool(name="work", bufs=3))
         psum = ctx.enter_context(tc.psum_pool(name="psum", bufs=2))
+        ctx.enter_context(tc.manual_schedule())
 
         ident = keep.tile([P, P], F32, name="ident")
         rho_row = keep.tile([P, 512], BF16, name="rho_row")
@@ -39,8 +57,8 @@ def tile_admm_kkt_step_s9_kernel(tc, z, y, rho, a_words, a_scales, c, kkt_inv, x
         k_codes = keep.tile([P, G2, N], U32, name="k_codes", align_bytes=64)
         k_sc = keep.tile([P, G2, N], U8, name="k_sc", align_bytes=64)
         k_raw = [keep.tile([P, 4, N], BF16, name="k_raw%d" % h) for h in range(G2)]
-        z_sb = [keep.tile([P, M], BF16, name="z%d" % i) for i in range(TILES)]
-        y_sb = [keep.tile([P, M], BF16, name="y%d" % i) for i in range(TILES)]
+        z_sb = [keep.tile([P, 2, M], BF16, name="z%d" % i) for i in range(PAIRS)]
+        y_sb = [keep.tile([P, 2, M], BF16, name="y%d" % i) for i in range(PAIRS)]
         c_sb = [keep.tile([P, N], BF16, name="c%d" % i) for i in range(TILES)]
         x_sb = [keep.tile([P, N], BF16, name="x%d" % i) for i in range(TILES)]
 
@@ -51,49 +69,33 @@ def tile_admm_kkt_step_s9_kernel(tc, z, y, rho, a_words, a_scales, c, kkt_inv, x
         def rows(i):
             return slice(i * P, (i + 1) * P)
 
-        def load_zy(i):
-            nc.sync.dma_start(out=z_sb[i][:], in_=z[rows(i), :])
-            nc.sync.dma_start(out=y_sb[i][:], in_=y[rows(i), :])
-
-        def load_c(i):
-            nc.sync.dma_start(out=c_sb[i][:], in_=c[rows(i), :])
-
-        def load_x(i):
-            nc.sync.dma_start(out=x_sb[i][:], in_=x[rows(i), :])
-
-        def load_k(h):
-            nc.sync.dma_start(
-                out=k_raw[h][:],
-                in_=kkt_inv[512 * h : 512 * (h + 1), :].rearrange("(p j) w -> p j w", j=4),
-            )
-
         nc.sync.dma_start(out=rho_row[0:G1, :], in_=rho.rearrange("(g k) -> g k", g=G1))
-        for half in range(2):
-            cols = slice(half * 1024, (half + 1) * 1024)
-            nc.sync.dma_start(out=z_sb[0][:, cols], in_=z[rows(0), cols])
-            nc.sync.dma_start(out=y_sb[0][:, cols], in_=y[rows(0), cols])
-        load_zy(1)
-        for r in range(4):
-            nc.sync.dma_start(
-                out=a_sc[r:P:32].bitcast(I32),
-                in_=a_scales[:, r:16:4, :].rearrange("g q n -> q g n").bitcast(I32),
-            )
-        for g in range(G1):
-            nc.sync.dma_start(out=a_sb[:, g, :], in_=a_words[g])
-        load_c(0)
-        load_zy(2)
-        load_k(0)
-        load_zy(3)
-        load_c(1)
-        load_k(1)
-        load_c(2)
-        for i in range(4, TILES):
-            load_zy(i)
-            load_c(i - 1)
-            load_x(i - 4)
-        load_c(TILES - 1)
-        for i in range(TILES - 4, TILES):
-            load_x(i)
+        for item in LOADS.split():
+            i = int(item[1]) if len(item) > 1 else 0
+            if item[0] == "Z":
+                cols = slice(1024 * int(item[2]), 1024 * (int(item[2]) + 1))
+                for dst, src in ((z_sb[i], z), (y_sb[i], y)):
+                    nc.sync.dma_start(
+                        out=dst[:, :, cols],
+                        in_=src[2 * P * i : 2 * P * (i + 1), cols].rearrange("(t p) k -> p t k", t=2),
+                    )
+            if item[0] == "A":
+                for r in range(4):
+                    nc.sync.dma_start(
+                        out=a_sc[r:P:32].bitcast(I32),
+                        in_=a_scales[:, r:16:4, :].rearrange("g q n -> q g n").bitcast(I32),
+                    )
+                for g in range(G1):
+                    nc.sync.dma_start(out=a_sb[:, g, :], in_=a_words[g])
+            if item[0] == "c":
+                nc.sync.dma_start(out=c_sb[i][:], in_=c[rows(i), :])
+            if item[0] == "x":
+                nc.sync.dma_start(out=x_sb[i][:], in_=x[rows(i), :])
+            if item[0] == "k":
+                nc.sync.dma_start(
+                    out=k_raw[i][:],
+                    in_=kkt_inv[512 * i : 512 * (i + 1), :].rearrange("(p j) w -> p j w", j=4),
+                )
 
         rho_t = psum.tile([P, 512], F32, name="acc2")
         for u in range(2):
@@ -105,150 +107,138 @@ def tile_admm_kkt_step_s9_kernel(tc, z, y, rho, a_words, a_scales, c, kkt_inv, x
             in_=rho_t[:, 0:256].bitcast(BF16).rearrange("p (u r e) -> p r u e", u=2, e=2)[:, 0:G1],
         )
 
-        v_codes, v_sc = {}, {}
-        v_half, r_bf, x06, acc1, acc2, r_codes, r_sc = {}, {}, {}, {}, {}, {}, {}
-        zt, yt, zr = {}, {}, {}
+        zt, yt, zr, vh, v_codes, v_sc, acc1, r_bf, r_t, r_il = {}, {}, {}, {}, {}, {}, {}, {}, {}, {}
+        r_codes, r_sc, acc2, x06, k_il = {}, {}, {}, {}, {}
 
-        def transpose_half(i, a):
-            zt[i, a] = psum.tile([P, 512], F32, name="zt")
-            yt[i, a] = psum.tile([P, 512], F32, name="yt")
-            for src, dst in ((z_sb[i], zt[i, a]), (y_sb[i], yt[i, a])):
-                words = src[:].bitcast(F32)
-                for gl in range(2):
-                    for u in range(2):
-                        base = 256 * (2 * a + gl)
-                        k = 2 * u + gl
-                        nc.tensor.transpose(
-                            dst[:, k * P : (k + 1) * P], words[:, base + u : base + 256 : 2], ident[:]
-                        )
-
-        def scale_half(i, a):
-            zr[i, a] = work.tile([P, 4, 2, P], F32, name="zr")
-            src = zt[i, a][:].bitcast(BF16).rearrange("p (u g b e) -> p g u e b", g=2, u=2, e=2)
-            for gl in range(2):
-                for t in range(4):
-                    nc.scalar.activation(
-                        out=zr[i, a][:, t, gl, :],
-                        in_=src[:, gl, t // 2, t % 2, :],
-                        func=COPY,
-                        scale=rho_col[:, 2 * a + gl, t : t + 1],
+        def words_t(src, dst, g):
+            for u in range(2):
+                for b in range(2):
+                    k = 2 * u + b
+                    nc.tensor.transpose(
+                        dst[:, k * P : (k + 1) * P],
+                        src[:, b, :].bitcast(F32)[:, 256 * g + u : 256 * (g + 1) : 2],
+                        ident[:],
                     )
 
-        def sub_half(i, a):
-            v_half[i, a] = work.tile([P, 2, P * 4], BF16, name="v_half", bufs=4, align_bytes=64)
+        def do_tz(p, g):
+            zt[p, g] = psum.tile([P, 512], F32, name="zt")
+            words_t(z_sb[p], zt[p, g], g)
+
+        def do_ty(p, g):
+            yt[p, g] = psum.tile([P, 512], F32, name="yt")
+            words_t(y_sb[p], yt[p, g], g)
+
+        def do_zr(p, g, t):
+            if t == 0:
+                zr[p, g] = work.tile([P, 4, 2 * P], F32, name="zr")
+            nc.scalar.activation(
+                out=zr[p, g][:, t, :],
+                in_=zt[p, g][:].bitcast(BF16).rearrange("p (u q e) -> p u e q", u=2, e=2)[:, t // 2, t % 2],
+                func=COPY,
+                scale=rho_col[:, g, t : t + 1],
+            )
+
+        def do_v(p, g):
+            vh[p, g] = work.tile([P, 8 * P], BF16, name="vh", bufs=4, align_bytes=64)
             nc.vector.tensor_tensor(
-                out=v_half[i, a][:].rearrange("p g (b u e) -> p (g b) u e", u=2, e=2),
-                in0=zr[i, a][:].rearrange("p (u e) g b -> p (g b) u e", e=2),
-                in1=yt[i, a][:].bitcast(BF16).rearrange("p (u q e) -> p q u e", u=2, e=2),
+                out=vh[p, g][:].rearrange("p (q u e) -> p q u e", u=2, e=2),
+                in0=zr[p, g][:].rearrange("p (u e) q -> p q u e", e=2),
+                in1=yt[p, g][:].bitcast(BF16).rearrange("p (u q e) -> p q u e", u=2, e=2),
                 op=SUB,
             )
 
-        def quant_v(i, a):
-            if a == 0:
-                v_codes[i] = work.tile([P, G1, P], U32, name="v_codes", align_bytes=64)
-                v_sc[i] = work.tile([P, G1, P], U8, name="v_sc", align_bytes=64)
-            gs = slice(2 * a, 2 * a + 2)
+        def do_qv(p, g):
+            v_codes[p, g] = work.tile([P, 2 * P], U32, name="v_codes", bufs=10, align_bytes=64)
+            v_sc[p, g] = work.tile([P, 2 * P], U8, name="v_sc", bufs=10, align_bytes=64)
             nc.vector.quantize_mx(
-                out=v_codes[i][:, gs, :].rearrange("p g b -> p (g b)").bitcast(E4M3),
-                scales=v_sc[i][:, gs, :].rearrange("p g b -> p (g b)"),
-                in_=v_half[i, a][:].rearrange("p g q -> p (g q)"),
+                out=v_codes[p, g][:].bitcast(E4M3), scales=v_sc[p, g][:], in_=vh[p, g][:]
             )
 
-        def mm1(i, h):
-            acc1[i, h] = psum.tile([P, 512], F32, name="acc1")
+        def do_m1(k):
+            p, b, h = k // 4, (k % 4) // 2, k % 2
+            acc1[k] = psum.tile([P, 512], F32, name="acc1")
             for g in range(G1):
                 nc.tensor.matmul_mx(
-                    out=acc1[i, h][:],
-                    lhsT=v_codes[i][:, g, :].bitcast(E4M3),
-                    lhsT_scale=v_sc[i][:, g, :],
+                    out=acc1[k][:],
+                    lhsT=v_codes[p, g][:, b * P : (b + 1) * P].bitcast(E4M3),
+                    lhsT_scale=v_sc[p, g][:, b * P : (b + 1) * P],
                     rhs=a_sb[:, g, 1024 * h : 1024 * (h + 1)].bitcast(E2M1),
                     rhs_scale=a_sc[:, g, 512 * h : 512 * (h + 1)],
                     start=(g == 0),
                     stop=(g == G1 - 1),
                 )
 
-        def residual(i, h):
+        def do_r(k):
+            i, h = k // 2, k % 2
             if h == 0:
-                r_bf[i] = work.tile([P, N], BF16, name="r_bf", bufs=5, align_bytes=64)
+                r_bf[i] = work.tile([P, N], BF16, name="r_bf", bufs=6, align_bytes=64)
             cols = slice(512 * h, 512 * (h + 1))
             nc.vector.tensor_tensor(
                 out=r_bf[i][:, cols].rearrange("p (u q e) -> p u q e", u=2, e=2),
-                in0=acc1[i, h][:].rearrange("p (q u e) -> p u q e", u=2, e=2),
+                in0=acc1[k][:].rearrange("p (q u e) -> p u q e", u=2, e=2),
                 in1=c_sb[i][:, cols].rearrange("p (q u e) -> p u q e", u=2, e=2),
                 op=SUB,
             )
 
-        r_t, r_il = {}, {}
-
-        def transpose_r(i):
-            r_t[i] = psum.tile([P, 512], F32, name="zt" if i >= 5 else "acc2")
+        def do_rt(i):
+            r_t[i] = psum.tile([P, 512], F32, name="acc2")
             words = r_bf[i][:].bitcast(F32)
             for k in range(4):
-                nc.tensor.transpose(
-                    r_t[i][:, k * P : (k + 1) * P], words[:, k * P : (k + 1) * P], ident[:]
-                )
+                nc.tensor.transpose(r_t[i][:, k * P : (k + 1) * P], words[:, k * P : (k + 1) * P], ident[:])
 
-        def copy_r(i):
-            r_il[i] = work.tile([P, 512, 2], BF16, name="r_il", bufs=2, align_bytes=64)
+        def do_rc(i):
+            r_il[i] = work.tile([P, N], BF16, name="r_il", bufs=2, align_bytes=64)
             nc.scalar.copy(
-                out=r_il[i][:].rearrange("p q e -> p (q e)").bitcast(F32).rearrange("p (h b u) -> p h b u", h=2, u=2),
+                out=r_il[i][:].bitcast(F32).rearrange("p (h b u) -> p h b u", h=2, u=2),
                 in_=r_t[i][:].rearrange("p (h u b) -> p h b u", h=2, u=2),
             )
 
-        def quant_r(i):
+        def do_qr(i):
             r_codes[i] = work.tile([P, G2 * P], U32, name="r_codes", bufs=4, align_bytes=64)
             r_sc[i] = work.tile([P, G2 * P], U8, name="r_sc", bufs=4, align_bytes=64)
-            nc.vector.quantize_mx(
-                out=r_codes[i][:].bitcast(E5M2),
-                scales=r_sc[i][:],
-                in_=r_il[i][:].rearrange("p q e -> p (q e)"),
-            )
+            nc.vector.quantize_mx(out=r_codes[i][:].bitcast(E5M2), scales=r_sc[i][:], in_=r_il[i][:])
 
-        def mm2(i):
-            for n in range(2):
-                acc2[i, n] = psum.tile([P, 512], F32, name="yt" if i == 6 else "acc2")
-                for h in range(G2):
-                    nc.tensor.matmul_mx(
-                        out=acc2[i, n][:],
-                        lhsT=r_codes[i][:, h * P : (h + 1) * P].bitcast(E5M2),
-                        lhsT_scale=r_sc[i][:, h * P : (h + 1) * P],
-                        rhs=k_codes[:, h, 512 * n : 512 * (n + 1)].bitcast(E4M3),
-                        rhs_scale=k_sc[:, h, 512 * n : 512 * (n + 1)],
-                        start=(h == 0),
-                        stop=(h == G2 - 1),
-                    )
+        def do_m2(i, n):
+            acc2[i, n] = psum.tile([P, 512], F32, name="acc2")
+            for h in range(G2):
+                nc.tensor.matmul_mx(
+                    out=acc2[i, n][:],
+                    lhsT=r_codes[i][:, h * P : (h + 1) * P].bitcast(E5M2),
+                    lhsT_scale=r_sc[i][:, h * P : (h + 1) * P],
+                    rhs=k_codes[:, h, 512 * n : 512 * (n + 1)].bitcast(E4M3),
+                    rhs_scale=k_sc[:, h, 512 * n : 512 * (n + 1)],
+                    start=(h == 0),
+                    stop=(h == G2 - 1),
+                )
 
-        def scale_x(i):
+        def do_x(i):
             x06[i] = work.tile([P, N], F32, name="x06", bufs=3)
             nc.scalar.activation(out=x06[i][:], in_=x_sb[i][:], func=COPY, scale=-0.6)
 
-        def finish(i):
-            for n in range(2):
-                cols = slice(512 * n, 512 * (n + 1))
-                o = work.tile([P, 512], F32, name="o", bufs=6)
-                nc.vector.scalar_tensor_tensor(
-                    out=o[:], in0=acc2[i, n][:], scalar=1.6, in1=x06[i][:, cols], op0=MULT, op1=ADD
-                )
-                nc.sync.dma_start(out=out[rows(i), cols], in_=o[:])
+        def do_o(i, n):
+            cols = slice(512 * n, 512 * (n + 1))
+            o = work.tile([P, 512], F32, name="o", bufs=5)
+            nc.vector.scalar_tensor_tensor(
+                out=o[:], in0=acc2[i, n][:], scalar=1.6, in1=x06[i][:, cols], op0=MULT, op1=ADD
+            )
+            nc.sync.dma_start(out=out[rows(i), cols], in_=o[:])
 
-        k_il = {}
-
-        def inter_k(h, n, part):
+        def do_ik(h, n, part, eng):
             if part == 0:
-                k_il[h, n] = work.tile([P, 512, 4], BF16, name="k_il", bufs=4, align_bytes=64)
+                k_il[h, n] = work.tile([P, 512, 4], BF16, name="k_il", bufs=3, align_bytes=64)
             w0 = 256 * part
-            dst = k_il[h, n][:, w0 : w0 + 256, :].rearrange("p (c i) t -> p c t i", i=4)
-            src = k_raw[h][:, :, 512 * n + w0 : 512 * n + w0 + 256].rearrange("p t (c i) -> p c t i", i=4)
-            if (h + n) % 2 == 0:
-                nc.scalar.copy(out=dst, in_=src)
+            src = k_raw[h][:, :, 512 * n + w0 : 512 * n + w0 + 256]
+            dst = k_il[h, n][:, w0 : w0 + 256, :]
+            if eng == "S":
+                nc.scalar.copy(
+                    out=dst.rearrange("p (c i) t -> p c t i", i=4), in_=src.rearrange("p t (c i) -> p c t i", i=4)
+                )
             else:
                 nc.gpsimd.tensor_scalar(
-                    out=k_il[h, n][:, w0 : w0 + 256, :],
-                    in0=k_raw[h][:, :, 512 * n + w0 : 512 * n + w0 + 256].rearrange("p t w -> p w t"),
-                    scalar1=1.0, scalar2=0.0, op0=MULT, op1=ADD,
+                    out=dst, in0=src.rearrange("p t w -> p w t"), scalar1=1.0, scalar2=0.0, op0=MULT, op1=ADD
                 )
 
-        def quant_k(h, n):
+        def do_qk(h, n):
             cols = slice(512 * n, 512 * (n + 1))
             nc.vector.quantize_mx(
                 out=k_codes[:, h, cols].bitcast(E4M3),
@@ -256,60 +246,34 @@ def tile_admm_kkt_step_s9_kernel(tc, z, y, rho, a_words, a_scales, c, kkt_inv, x
                 in_=k_il[h, n][:].rearrange("p w t -> p (w t)"),
             )
 
-        for a in range(2):
-            transpose_half(0, a)
-            scale_half(0, a)
-        for a in range(2):
-            sub_half(0, a)
-        for a in range(2):
-            quant_v(0, a)
-
-        for s in range(TILES):
-            nxt = s + 1
-            if s >= 5:
-                finish(1 if s == 5 else s - 4)
-            if nxt < TILES:
-                for a in range(2):
-                    transpose_half(nxt, a)
-                    scale_half(nxt, a)
-                    sub_half(nxt, a)
-            for j in [0, 1] if s == 3 else [s - 2] if s >= 4 else []:
-                transpose_r(j)
-                copy_r(j)
-                quant_r(j)
-            if s == 4:
-                mm2(0)
-                finish(0)
-            mm1(s, 0)
-            mm1(s, 1)
-            residual(s, 0)
-            if nxt < TILES:
-                quant_v(nxt, 0)
-            residual(s, 1)
-            if nxt < TILES:
-                quant_v(nxt, 1)
-            if s == 1 or s == 2:
-                for n in range(2):
-                    for part in range(2):
-                        inter_k(s - 1, n, part)
-            if s == 2:
-                quant_k(0, 0)
-            if s == 3:
-                quant_k(0, 1)
-                quant_k(1, 0)
-                quant_k(1, 1)
-                scale_x(0)
-                scale_x(1)
-            if s >= 4:
-                mm2(1 if s == 4 else s - 3)
-                scale_x(s - 2)
-        finish(4)
-        for j in (6, 7):
-            transpose_r(j)
-            copy_r(j)
-            quant_r(j)
-            mm2(j - 1)
-            scale_x(j)
-            finish(j - 1)
-        mm2(7)
-        finish(7)
+        for tok in ORDER.split():
+            if tok.startswith("Tz"):
+                do_tz(int(tok[2]), int(tok[3]))
+            elif tok.startswith("Ty"):
+                do_ty(int(tok[2]), int(tok[3]))
+            elif tok.startswith("zr"):
+                do_zr(int(tok[2]), int(tok[3]), int(tok[4]))
+            elif tok.startswith("v"):
+                do_v(int(tok[1]), int(tok[2]))
+            elif tok.startswith("qv"):
+                do_qv(int(tok[2]), int(tok[3]))
+            elif tok.startswith("M1_"):
+                do_m1(int(tok[3:]))
+            elif tok.startswith("M2_"):
+                do_m2(int(tok[3]), int(tok[4]))
+            elif tok.startswith("rT"):
+                do_rt(int(tok[2]))
+            elif tok.startswith("rc"):
+                do_rc(int(tok[2]))
+            elif tok.startswith("r"):
+                do_r(int(tok[1:]))
+            elif tok.startswith("qr"):
+                do_qr(int(tok[2]))
+            elif tok.startswith("x06_"):
+                do_x(int(tok[4]))
+            elif tok.startswith("o"):
+                do_o(int(tok[1]), int(tok[2]))
+            elif tok.startswith("ik"):
+                do_ik(int(tok[2]), int(tok[3]), int(tok[4]), tok[5])
+            elif tok.startswith("qk"):
+                do_qk(int(tok[2]), int(tok[3]))

@@ -18,26 +18,23 @@ SUB = mybir.AluOpType.subtract
 
 P = 128
 B, M, N = 1024, 2048, 1024
-PAIRS = B // (2 * P)
 TILES = B // P
 G1 = M // 512
 G2 = N // 512
 FLOPS = 2 * B * M * N + 2 * B * N * N
-LOADS = "Z00 Z01 Z10 Z11 A c0 c1 k0 c2 k1 Z20 Z21 c3 x0 x1 c4 c5 Z30 Z31 x2 x3 c6 c7 x4 x5 x6 x7"
+LOADS = "Z0 Z1 Z2 A c0 c1 Z3 k0 c2 k1 Z4 c3 x0 Z5 c4 x1 Z6 c5 x2 Z7 c6 x3 c7 x4 x5 x6 x7"
 ORDER = (
-    "Tz00 Tz01 zr000 zr001 Ty00 zr002 zr003 Ty01 zr010 v00 zr011 Tz02 zr012 zr013 zr020 Ty02 qv00 "
-    "zr021 v01 zr022 Tz03 zr023 zr030 Tz10 v02 zr031 Ty03 zr032 zr033 zr100 qv01 Ty10 zr101 qv02 "
-    "zr102 Tz11 v03 zr103 Tz12 zr110 zr111 v10 Ty11 zr112 zr113 zr120 Tz13 qv03 zr121 qv10 zr122 Ty12 "
-    "zr123 v11 zr130 zr131 zr132 M1_0 v12 zr133 qv11 Ty13 qv12 M1_1 r0 v13 M1_2 ik000S r1 qv13 M1_3 "
-    "r2 ik001S M1_4 r3 ik010S qk00 ik100G M1_5 r4 ik011S ik101G Tz20 r5 Tz21 zr200 qk01 Ty20 zr201 "
-    "ik110G zr202 Ty21 qk10 zr203 rT0 zr210 v20 Tz22 ik111G rc0 M1_6 zr211 qr0 zr212 qv20 zr213 qk11 "
-    "zr220 Ty22 zr221 v21 zr222 M2_00 zr223 x06_0 M2_01 v22 Tz23 x06_1 Ty23 qv21 qv22 Tz30 o00 zr230 "
-    "M1_7 zr231 o01 zr232 zr233 r6 zr300 Ty30 zr301 v23 zr302 Tz31 zr303 rT1 zr310 Tz32 v30 rc1 Ty31 "
-    "zr311 rT2 zr312 qv23 Ty32 qv30 rc2 qr1 M1_8 zr313 r7 zr320 zr321 qr2 M2_10 zr322 v31 zr323 M2_11 "
-    "x06_2 o10 Tz33 Ty33 qv31 zr330 o11 zr331 M2_20 zr332 r8 zr333 M2_21 x06_3 v32 M1_9 x06_4 o20 "
-    "M1_10 qv32 r9 rT3 o21 M1_11 rc3 v33 x06_5 rT4 qr3 rc4 qv33 M2_30 r10 M2_31 r11 M1_12 qr4 o30 "
-    "M1_13 o31 r12 x06_6 M2_40 r13 M2_41 o40 M1_14 o41 M1_15 x06_7 r14 rT5 r15 rT6 rc5 rc6 rT7 qr5 "
-    "rc7 M2_50 qr6 M2_51 o50 o51 M2_60 qr7 M2_61 o60 o61 M2_70 M2_71 o70 o71 "
+    "Tz0 Ty0 zr00 zr01 vm0 v0 gs00 Tz1 zr10 vm1 gs01 Ty1 zr11 qv00 Tn0 v1 gs10 Tz2 cp0 zr20 gs11 vm2 "
+    "Ty2 zr21 qv01 Tn1 qv10 cp1 v2 gs20 M1_00 gs21 M1_01 qv11 qv20 r00 Tn2 r01 Tz3 cp2 vm3 M1_10 zr30 "
+    "zr31 qv21 Ty3 r10 gs30 rT0 v3 M1_11 rc0 gs31 ik000S M1_20 qv30 r11 ik001S Tn3 r20 rT1 qr0 M1_21 "
+    "cp3 qk00 ik010S qv31 ik100G Tz4 vm4 M1_30 zr40 ik101G r21 zr41 Ty4 r30 ik011S gs40 rT2 v4 M1_31 "
+    "x06_0 gs41 vm5 Tz5 rc1 ik110G Tn4 r31 Ty5 cp4 rT3 zr50 qv40 qv41 qr1 zr51 M1_40 qk01 x06_1 qk10 "
+    "Tz6 r40 ik111G rc2 M1_41 v5 zr60 gs50 M2_00 zr61 vm6 Ty6 x06_2 gs51 Tz7 o00 rc3 gs60 r41 Tn5 "
+    "M2_10 v6 cp5 gs61 zr70 rT4 o10 Ty7 zr71 qv50 Tn6 qv51 cp6 qv60 M1_50 qk11 qv61 M2_01 qr2 r50 "
+    "M1_51 rc4 o01 M2_11 vm7 x06_3 M2_20 M1_60 o11 gs70 o20 x06_4 M2_21 r51 gs71 o21 rT5 qr3 Tn7 "
+    "x06_5 r60 M2_30 v7 M1_61 cp7 rc5 qv71 qv70 M2_31 o30 M1_70 o31 r61 x06_6 qr4 rT6 r70 M2_40 rc6 "
+    "qr5 M1_71 o40 qr6 M2_41 r71 M2_50 o41 o50 M2_51 x06_7 rT7 o51 rc7 M2_60 qr7 M2_61 o60 o61 M2_70 "
+    "M2_71 o70 o71 "
 )
 
 
@@ -57,8 +54,8 @@ def tile_admm_kkt_step_s9_kernel(tc, z, y, rho, a_words, a_scales, c, kkt_inv, x
         k_codes = keep.tile([P, G2, N], U32, name="k_codes", align_bytes=64)
         k_sc = keep.tile([P, G2, N], U8, name="k_sc", align_bytes=64)
         k_raw = [keep.tile([P, 4, N], BF16, name="k_raw%d" % h) for h in range(G2)]
-        z_sb = [keep.tile([P, 2, M], BF16, name="z%d" % i) for i in range(PAIRS)]
-        y_sb = [keep.tile([P, 2, M], BF16, name="y%d" % i) for i in range(PAIRS)]
+        z_sb = [keep.tile([P, M], BF16, name="z%d" % i) for i in range(TILES)]
+        y_sb = [keep.tile([P, M], BF16, name="y%d" % i) for i in range(TILES)]
         c_sb = [keep.tile([P, N], BF16, name="c%d" % i) for i in range(TILES)]
         x_sb = [keep.tile([P, N], BF16, name="x%d" % i) for i in range(TILES)]
 
@@ -73,12 +70,9 @@ def tile_admm_kkt_step_s9_kernel(tc, z, y, rho, a_words, a_scales, c, kkt_inv, x
         for item in LOADS.split():
             i = int(item[1]) if len(item) > 1 else 0
             if item[0] == "Z":
-                cols = slice(1024 * int(item[2]), 1024 * (int(item[2]) + 1))
-                for dst, src in ((z_sb[i], z), (y_sb[i], y)):
-                    nc.sync.dma_start(
-                        out=dst[:, :, cols],
-                        in_=src[2 * P * i : 2 * P * (i + 1), cols].rearrange("(t p) k -> p t k", t=2),
-                    )
+                for cols in (slice(0, 1024), slice(1024, 2048)) if i == 0 else (slice(0, 2048),):
+                    for dst, src in ((z_sb[i], z), (y_sb[i], y)):
+                        nc.sync.dma_start(out=dst[:, cols], in_=src[rows(i), cols])
             if item[0] == "A":
                 for r in range(4):
                     nc.sync.dma_start(
@@ -107,71 +101,121 @@ def tile_admm_kkt_step_s9_kernel(tc, z, y, rho, a_words, a_scales, c, kkt_inv, x
             in_=rho_t[:, 0:256].bitcast(BF16).rearrange("p (u r e) -> p r u e", u=2, e=2)[:, 0:G1],
         )
 
+        rho_w = keep.tile([P, G1, 2], F32, name="rho_w")
+        rho_ps = psum.tile([P, 512], F32, name="rho_ps", bufs=1)
+        nc.vector.tensor_copy(
+            out=rho_w[:], in_=rho_t[:, 0:256].rearrange("p (u r) -> p r u", u=2)[:, 0:G1]
+        )
+        for k in range(4):
+            nc.tensor.transpose(
+                rho_ps[:, k * P : (k + 1) * P],
+                rho_w[:, 2 + k % 2, k // 2 : k // 2 + 1].to_broadcast([P, P]),
+                ident[:],
+            )
+
+        zn, vn, vt, scaled = {}, {}, {}, {}
         zt, yt, zr, vh, v_codes, v_sc, acc1, r_bf, r_t, r_il = {}, {}, {}, {}, {}, {}, {}, {}, {}, {}
         r_codes, r_sc, acc2, x06, k_il = {}, {}, {}, {}, {}
 
-        def words_t(src, dst, g):
+        def words_t(src, dst):
             for u in range(2):
-                for b in range(2):
-                    k = 2 * u + b
+                for g in range(2):
+                    k = 2 * u + g
                     nc.tensor.transpose(
                         dst[:, k * P : (k + 1) * P],
-                        src[:, b, :].bitcast(F32)[:, 256 * g + u : 256 * (g + 1) : 2],
+                        src[:].bitcast(F32)[:, 256 * g + u : 256 * (g + 1) : 2],
                         ident[:],
                     )
 
-        def do_tz(p, g):
-            zt[p, g] = psum.tile([P, 512], F32, name="zt")
-            words_t(z_sb[p], zt[p, g], g)
+        def do_tz(i):
+            zt[i] = psum.tile([P, 512], F32, name="zt", bufs=1)
+            words_t(z_sb[i], zt[i])
 
-        def do_ty(p, g):
-            yt[p, g] = psum.tile([P, 512], F32, name="yt")
-            words_t(y_sb[p], yt[p, g], g)
+        def do_ty(i):
+            yt[i] = psum.tile([P, 512], F32, name="yt", bufs=1)
+            words_t(y_sb[i], yt[i])
 
-        def do_zr(p, g, t):
-            if t == 0:
-                zr[p, g] = work.tile([P, 4, 2 * P], F32, name="zr")
-            nc.scalar.activation(
-                out=zr[p, g][:, t, :],
-                in_=zt[p, g][:].bitcast(BF16).rearrange("p (u q e) -> p u e q", u=2, e=2)[:, t // 2, t % 2],
-                func=COPY,
-                scale=rho_col[:, g, t : t + 1],
-            )
+        def do_zr(i, g):
+            if g == 0:
+                zr[i] = work.tile([P, 4, 2, P], F32, name="zr", bufs=2)
+            src = zt[i][:].bitcast(BF16).rearrange("p (u g b e) -> p u e g b", u=2, g=2, e=2)
+            for t in range(4):
+                nc.scalar.activation(
+                    out=zr[i][:, t, g, :],
+                    in_=src[:, t // 2, t % 2, g],
+                    func=COPY,
+                    scale=rho_col[:, g, t : t + 1],
+                )
 
-        def do_v(p, g):
-            vh[p, g] = work.tile([P, 8 * P], BF16, name="vh", bufs=4, align_bytes=64)
+        def do_v(i):
+            vh[i, 0] = work.tile([P, 8 * P], BF16, name="vh", bufs=5, align_bytes=64)
             nc.vector.tensor_tensor(
-                out=vh[p, g][:].rearrange("p (q u e) -> p q u e", u=2, e=2),
-                in0=zr[p, g][:].rearrange("p (u e) q -> p q u e", e=2),
-                in1=yt[p, g][:].bitcast(BF16).rearrange("p (u q e) -> p q u e", u=2, e=2),
+                out=vh[i, 0][:].rearrange("p (q u e) -> p q u e", u=2, e=2),
+                in0=zr[i][:].rearrange("p (u e) g b -> p (g b) u e", e=2),
+                in1=yt[i][:].bitcast(BF16).rearrange("p (u q e) -> p q u e", u=2, e=2),
                 op=SUB,
             )
 
-        def do_qv(p, g):
-            v_codes[p, g] = work.tile([P, 2 * P], U32, name="v_codes", bufs=10, align_bytes=64)
-            v_sc[p, g] = work.tile([P, 2 * P], U8, name="v_sc", bufs=10, align_bytes=64)
-            nc.vector.quantize_mx(
-                out=v_codes[p, g][:].bitcast(E4M3), scales=v_sc[p, g][:], in_=vh[p, g][:]
+        def do_vm(i):
+            zn[i] = work.tile([P, 1024], F32, name="zn", bufs=2)
+            nc.vector.tensor_tensor(
+                out=zn[i][:].rearrange("p (u q e) -> p u q e", u=2, e=2),
+                in0=z_sb[i][:, 1024:2048].rearrange("p (q u e) -> p u q e", u=2, e=2),
+                in1=rho_ps[:].bitcast(BF16).rearrange("p (u q e) -> p u q e", u=2, e=2),
+                op=MULT,
             )
 
-        def do_m1(k):
-            p, b, h = k // 4, (k % 4) // 2, k % 2
+        def do_gs(i, u):
+            if u == 0:
+                vn[i] = work.tile([P, 2, 512], BF16, name="vn", bufs=2, align_bytes=64)
+            nc.gpsimd.tensor_tensor(
+                out=vn[i][:, u, :].rearrange("p (q e) -> p q e", e=2),
+                in0=zn[i][:, 512 * u : 512 * (u + 1)].rearrange("p (q e) -> p q e", e=2),
+                in1=y_sb[i][:, 1024:2048].rearrange("p (q u e) -> p u q e", u=2, e=2)[:, u],
+                op=SUB,
+            )
+
+        def do_tn(i):
+            vt[i] = psum.tile([P, 512], F32, name="vt", bufs=1)
+            words = vn[i][:].rearrange("p u q -> p (u q)").bitcast(F32)
+            for k in range(4):
+                nc.tensor.transpose(vt[i][:, k * P : (k + 1) * P], words[:, k * P : (k + 1) * P], ident[:])
+
+        def do_cp(i):
+            vh[i, 1] = work.tile([P, 8 * P], BF16, name="vh", bufs=5, align_bytes=64)
+            nc.scalar.copy(
+                out=vh[i, 1][:].bitcast(F32).rearrange("p (q u) -> p q u", u=2),
+                in_=vt[i][:].rearrange("p (u q) -> p q u", u=2),
+            )
+
+        def do_qv(i, a):
+            if i not in v_codes:
+                v_codes[i] = work.tile([P, G1, P], U32, name="v_codes", bufs=3, align_bytes=64)
+                v_sc[i] = work.tile([P, G1, P], U8, name="v_sc", bufs=3, align_bytes=64)
+            nc.vector.quantize_mx(
+                out=v_codes[i][:, 2 * a : 2 * a + 2, :].rearrange("p g b -> p (g b)").bitcast(E4M3),
+                scales=v_sc[i][:, 2 * a : 2 * a + 2, :].rearrange("p g b -> p (g b)"),
+                in_=vh[i, a][:],
+            )
+
+        def do_m1(i, h):
+            k = 2 * i + h
             acc1[k] = psum.tile([P, 512], F32, name="acc1")
             for g in range(G1):
                 nc.tensor.matmul_mx(
                     out=acc1[k][:],
-                    lhsT=v_codes[p, g][:, b * P : (b + 1) * P].bitcast(E4M3),
-                    lhsT_scale=v_sc[p, g][:, b * P : (b + 1) * P],
+                    lhsT=v_codes[i][:, g, :].bitcast(E4M3),
+                    lhsT_scale=v_sc[i][:, g, :],
                     rhs=a_sb[:, g, 1024 * h : 1024 * (h + 1)].bitcast(E2M1),
                     rhs_scale=a_sc[:, g, 512 * h : 512 * (h + 1)],
                     start=(g == 0),
                     stop=(g == G1 - 1),
                 )
 
-        def do_r(k):
-            i, h = k // 2, k % 2
+        def do_r(i, h):
+            k = 2 * i + h
             if h == 0:
-                r_bf[i] = work.tile([P, N], BF16, name="r_bf", bufs=6, align_bytes=64)
+                r_bf[i] = work.tile([P, N], BF16, name="r_bf", bufs=5, align_bytes=64)
             cols = slice(512 * h, 512 * (h + 1))
             nc.vector.tensor_tensor(
                 out=r_bf[i][:, cols].rearrange("p (u q e) -> p u q e", u=2, e=2),
@@ -223,6 +267,15 @@ def tile_admm_kkt_step_s9_kernel(tc, z, y, rho, a_words, a_scales, c, kkt_inv, x
             )
             nc.sync.dma_start(out=out[rows(i), cols], in_=o[:])
 
+        def do_se(i):
+            scaled[i] = work.tile([P, 512], F32, name="scaled", bufs=2)
+            nc.scalar.activation(out=scaled[i][:], in_=acc2[i, 1][:], func=COPY, scale=1.6)
+
+        def do_ga(i):
+            o = work.tile([P, 512], F32, name="o", bufs=5)
+            nc.gpsimd.tensor_tensor(out=o[:], in0=scaled[i][:], in1=x06[i][:, 512:1024], op=ADD)
+            nc.sync.dma_start(out=out[rows(i), 512:1024], in_=o[:])
+
         def do_ik(h, n, part, eng):
             if part == 0:
                 k_il[h, n] = work.tile([P, 512, 4], BF16, name="k_il", bufs=3, align_bytes=64)
@@ -246,34 +299,19 @@ def tile_admm_kkt_step_s9_kernel(tc, z, y, rho, a_words, a_scales, c, kkt_inv, x
                 in_=k_il[h, n][:].rearrange("p w t -> p (w t)"),
             )
 
+        actions = {
+            "Tz": do_tz, "Ty": do_ty, "zr": do_zr, "v": do_v, "vm": do_vm, "gs": do_gs, "Tn": do_tn, "cp": do_cp,
+            "qv": do_qv, "M1_": do_m1, "r": do_r, "rT": do_rt, "rc": do_rc, "qr": do_qr, "M2_": do_m2,
+            "x06_": do_x, "o": do_o, "se": do_se, "ga": do_ga, "qk": do_qk,
+        }
         for tok in ORDER.split():
-            if tok.startswith("Tz"):
-                do_tz(int(tok[2]), int(tok[3]))
-            elif tok.startswith("Ty"):
-                do_ty(int(tok[2]), int(tok[3]))
-            elif tok.startswith("zr"):
-                do_zr(int(tok[2]), int(tok[3]), int(tok[4]))
-            elif tok.startswith("v"):
-                do_v(int(tok[1]), int(tok[2]))
-            elif tok.startswith("qv"):
-                do_qv(int(tok[2]), int(tok[3]))
-            elif tok.startswith("M1_"):
-                do_m1(int(tok[3:]))
-            elif tok.startswith("M2_"):
-                do_m2(int(tok[3]), int(tok[4]))
-            elif tok.startswith("rT"):
-                do_rt(int(tok[2]))
-            elif tok.startswith("rc"):
-                do_rc(int(tok[2]))
-            elif tok.startswith("r"):
-                do_r(int(tok[1:]))
-            elif tok.startswith("qr"):
-                do_qr(int(tok[2]))
-            elif tok.startswith("x06_"):
-                do_x(int(tok[4]))
-            elif tok.startswith("o"):
-                do_o(int(tok[1]), int(tok[2]))
-            elif tok.startswith("ik"):
+            if tok.startswith("ik"):
                 do_ik(int(tok[2]), int(tok[3]), int(tok[4]), tok[5])
-            elif tok.startswith("qk"):
-                do_qk(int(tok[2]), int(tok[3]))
+                continue
+            digits = "0123456789"
+            name = tok
+            args = []
+            while name[len(name) - 1] in digits and not (name == "x06_"):
+                args.append(int(name[len(name) - 1]))
+                name = name[: len(name) - 1]
+            actions[name](*reversed(args))

from contextlib import ExitStack

import concourse.mybir as mybir
from concourse.masks import make_identity

F32 = mybir.dt.float32
BF16 = mybir.dt.bfloat16
I32 = mybir.dt.int32
U32 = mybir.dt.uint32
U8 = mybir.dt.uint8
E4M3 = mybir.dt.float8_e4m3fn_x4
E5M2 = mybir.dt.float8_e5m2_x4
E2M1 = mybir.dt.float4_e2m1fn_x4
COPY = mybir.ActivationFunctionType.Copy
ADD = mybir.AluOpType.add
MULT = mybir.AluOpType.mult
SUB = mybir.AluOpType.subtract

P = 128
B, M, N = 1024, 2048, 1024
TILES = B // P
G1 = M // 512
G2 = N // 512
FLOPS = 2 * B * M * N + 2 * B * N * N
LOADS = "Z0 Z1 Z2 A c0 c1 Z3 k0 c2 k1 Z4 c3 x0 Z5 c4 x1 Z6 c5 x2 Z7 c6 x3 c7 x4 x5 x6 x7"
ORDER = (
    "Tz0 Ty0 zr00 zr01 vm0 v0 gs00 Tz1 zr10 vm1 gs01 Ty1 zr11 qv00 Tn0 v1 gs10 Tz2 cp0 zr20 gs11 vm2 "
    "Ty2 zr21 qv01 Tn1 qv10 cp1 v2 gs20 M1_00 gs21 M1_01 qv11 qv20 r00 Tn2 r01 Tz3 cp2 vm3 M1_10 zr30 "
    "zr31 qv21 Ty3 r10 gs30 rT0 v3 M1_11 rc0 gs31 ik000S M1_20 qv30 r11 ik001S Tn3 r20 rT1 qr0 M1_21 "
    "cp3 qk00 ik010S qv31 ik100G Tz4 vm4 M1_30 zr40 ik101G r21 zr41 Ty4 r30 ik011S gs40 rT2 v4 M1_31 "
    "x06_0 gs41 vm5 Tz5 rc1 ik110G Tn4 r31 Ty5 cp4 rT3 zr50 qv40 qv41 qr1 zr51 M1_40 qk01 x06_1 qk10 "
    "Tz6 r40 ik111G rc2 M1_41 v5 zr60 gs50 M2_00 zr61 vm6 Ty6 x06_2 gs51 Tz7 o00 rc3 gs60 r41 Tn5 "
    "M2_10 v6 cp5 gs61 zr70 rT4 o10 Ty7 zr71 qv50 Tn6 qv51 cp6 qv60 M1_50 qk11 qv61 M2_01 qr2 r50 "
    "M1_51 rc4 o01 M2_11 vm7 x06_3 M2_20 M1_60 o11 gs70 o20 x06_4 M2_21 r51 gs71 o21 rT5 qr3 Tn7 "
    "x06_5 r60 M2_30 v7 M1_61 cp7 rc5 qv71 qv70 M2_31 o30 M1_70 o31 r61 x06_6 qr4 rT6 r70 M2_40 rc6 "
    "qr5 M1_71 o40 qr6 M2_41 r71 M2_50 o41 o50 M2_51 x06_7 rT7 o51 rc7 M2_60 qr7 M2_61 o60 o61 M2_70 "
    "M2_71 o70 o71 "
)


def tile_admm_kkt_step_s9_kernel(tc, z, y, rho, a_words, a_scales, c, kkt_inv, x, out):
    nc = tc.nc
    with ExitStack() as ctx:
        keep = ctx.enter_context(tc.tile_pool(name="keep", bufs=1))
        work = ctx.enter_context(tc.tile_pool(name="work", bufs=3))
        psum = ctx.enter_context(tc.psum_pool(name="psum", bufs=2))
        ctx.enter_context(tc.manual_schedule())

        ident = keep.tile([P, P], F32, name="ident")
        rho_row = keep.tile([P, 512], BF16, name="rho_row")
        rho_col = keep.tile([P, G1, 4], F32, name="rho_col")
        a_sb = keep.tile([P, G1, 2 * N], U8, name="a_sb", align_bytes=64)
        a_sc = keep.tile([P, G1, N], U8, name="a_sc", align_bytes=64)
        k_codes = keep.tile([P, G2, N], U32, name="k_codes", align_bytes=64)
        k_sc = keep.tile([P, G2, N], U8, name="k_sc", align_bytes=64)
        k_raw = [keep.tile([P, 4, N], BF16, name="k_raw%d" % h) for h in range(G2)]
        z_sb = [keep.tile([P, M], BF16, name="z%d" % i) for i in range(TILES)]
        y_sb = [keep.tile([P, M], BF16, name="y%d" % i) for i in range(TILES)]
        c_sb = [keep.tile([P, N], BF16, name="c%d" % i) for i in range(TILES)]
        x_sb = [keep.tile([P, N], BF16, name="x%d" % i) for i in range(TILES)]

        make_identity(nc, ident[:])
        nc.vector.memset(rho_row[:], 0.0)
        nc.vector.memset(a_sc[:].rearrange("p g n -> p (g n)").bitcast(I32), 0)

        def rows(i):
            return slice(i * P, (i + 1) * P)

        nc.sync.dma_start(out=rho_row[0:G1, :], in_=rho.rearrange("(g k) -> g k", g=G1))
        for item in LOADS.split():
            i = int(item[1]) if len(item) > 1 else 0
            if item[0] == "Z":
                for cols in (slice(0, 1024), slice(1024, 2048)) if i == 0 else (slice(0, 2048),):
                    for dst, src in ((z_sb[i], z), (y_sb[i], y)):
                        nc.sync.dma_start(out=dst[:, cols], in_=src[rows(i), cols])
            if item[0] == "A":
                for r in range(4):
                    nc.sync.dma_start(
                        out=a_sc[r:P:32].bitcast(I32),
                        in_=a_scales[:, r:16:4, :].rearrange("g q n -> q g n").bitcast(I32),
                    )
                for g in range(G1):
                    nc.sync.dma_start(out=a_sb[:, g, :], in_=a_words[g])
            if item[0] == "c":
                nc.sync.dma_start(out=c_sb[i][:], in_=c[rows(i), :])
            if item[0] == "x":
                nc.sync.dma_start(out=x_sb[i][:], in_=x[rows(i), :])
            if item[0] == "k":
                nc.sync.dma_start(
                    out=k_raw[i][:],
                    in_=kkt_inv[512 * i : 512 * (i + 1), :].rearrange("(p j) w -> p j w", j=4),
                )

        rho_t = psum.tile([P, 512], F32, name="acc2")
        for u in range(2):
            nc.tensor.transpose(
                rho_t[:, u * P : (u + 1) * P], rho_row[:].bitcast(F32)[:, u:256:2], ident[:]
            )
        nc.vector.tensor_copy(
            out=rho_col[:].rearrange("p g (u e) -> p g u e", e=2),
            in_=rho_t[:, 0:256].bitcast(BF16).rearrange("p (u r e) -> p r u e", u=2, e=2)[:, 0:G1],
        )

        rho_w = keep.tile([P, G1, 2], F32, name="rho_w")
        rho_ps = psum.tile([P, 512], F32, name="rho_ps", bufs=1)
        nc.vector.tensor_copy(
            out=rho_w[:], in_=rho_t[:, 0:256].rearrange("p (u r) -> p r u", u=2)[:, 0:G1]
        )
        for k in range(4):
            nc.tensor.transpose(
                rho_ps[:, k * P : (k + 1) * P],
                rho_w[:, 2 + k % 2, k // 2 : k // 2 + 1].to_broadcast([P, P]),
                ident[:],
            )

        zn, vn, vt, scaled = {}, {}, {}, {}
        zt, yt, zr, vh, v_codes, v_sc, acc1, r_bf, r_t, r_il = {}, {}, {}, {}, {}, {}, {}, {}, {}, {}
        r_codes, r_sc, acc2, x06, k_il = {}, {}, {}, {}, {}

        def words_t(src, dst):
            for u in range(2):
                for g in range(2):
                    k = 2 * u + g
                    nc.tensor.transpose(
                        dst[:, k * P : (k + 1) * P],
                        src[:].bitcast(F32)[:, 256 * g + u : 256 * (g + 1) : 2],
                        ident[:],
                    )

        def do_tz(i):
            zt[i] = psum.tile([P, 512], F32, name="zt", bufs=1)
            words_t(z_sb[i], zt[i])

        def do_ty(i):
            yt[i] = psum.tile([P, 512], F32, name="yt", bufs=1)
            words_t(y_sb[i], yt[i])

        def do_zr(i, g):
            if g == 0:
                zr[i] = work.tile([P, 4, 2, P], F32, name="zr", bufs=2)
            src = zt[i][:].bitcast(BF16).rearrange("p (u g b e) -> p u e g b", u=2, g=2, e=2)
            for t in range(4):
                nc.scalar.activation(
                    out=zr[i][:, t, g, :],
                    in_=src[:, t // 2, t % 2, g],
                    func=COPY,
                    scale=rho_col[:, g, t : t + 1],
                )

        def do_v(i):
            vh[i, 0] = work.tile([P, 8 * P], BF16, name="vh", bufs=5, align_bytes=64)
            nc.vector.tensor_tensor(
                out=vh[i, 0][:].rearrange("p (q u e) -> p q u e", u=2, e=2),
                in0=zr[i][:].rearrange("p (u e) g b -> p (g b) u e", e=2),
                in1=yt[i][:].bitcast(BF16).rearrange("p (u q e) -> p q u e", u=2, e=2),
                op=SUB,
            )

        def do_vm(i):
            zn[i] = work.tile([P, 1024], F32, name="zn", bufs=2)
            nc.vector.tensor_tensor(
                out=zn[i][:].rearrange("p (u q e) -> p u q e", u=2, e=2),
                in0=z_sb[i][:, 1024:2048].rearrange("p (q u e) -> p u q e", u=2, e=2),
                in1=rho_ps[:].bitcast(BF16).rearrange("p (u q e) -> p u q e", u=2, e=2),
                op=MULT,
            )

        def do_gs(i, u):
            if u == 0:
                vn[i] = work.tile([P, 2, 512], BF16, name="vn", bufs=2, align_bytes=64)
            nc.gpsimd.tensor_tensor(
                out=vn[i][:, u, :].rearrange("p (q e) -> p q e", e=2),
                in0=zn[i][:, 512 * u : 512 * (u + 1)].rearrange("p (q e) -> p q e", e=2),
                in1=y_sb[i][:, 1024:2048].rearrange("p (q u e) -> p u q e", u=2, e=2)[:, u],
                op=SUB,
            )

        def do_tn(i):
            vt[i] = psum.tile([P, 512], F32, name="vt", bufs=1)
            words = vn[i][:].rearrange("p u q -> p (u q)").bitcast(F32)
            for k in range(4):
                nc.tensor.transpose(vt[i][:, k * P : (k + 1) * P], words[:, k * P : (k + 1) * P], ident[:])

        def do_cp(i):
            vh[i, 1] = work.tile([P, 8 * P], BF16, name="vh", bufs=5, align_bytes=64)
            nc.scalar.copy(
                out=vh[i, 1][:].bitcast(F32).rearrange("p (q u) -> p q u", u=2),
                in_=vt[i][:].rearrange("p (u q) -> p q u", u=2),
            )

        def do_qv(i, a):
            if i not in v_codes:
                v_codes[i] = work.tile([P, G1, P], U32, name="v_codes", bufs=3, align_bytes=64)
                v_sc[i] = work.tile([P, G1, P], U8, name="v_sc", bufs=3, align_bytes=64)
            nc.vector.quantize_mx(
                out=v_codes[i][:, 2 * a : 2 * a + 2, :].rearrange("p g b -> p (g b)").bitcast(E4M3),
                scales=v_sc[i][:, 2 * a : 2 * a + 2, :].rearrange("p g b -> p (g b)"),
                in_=vh[i, a][:],
            )

        def do_m1(i, h):
            k = 2 * i + h
            acc1[k] = psum.tile([P, 512], F32, name="acc1")
            for g in range(G1):
                nc.tensor.matmul_mx(
                    out=acc1[k][:],
                    lhsT=v_codes[i][:, g, :].bitcast(E4M3),
                    lhsT_scale=v_sc[i][:, g, :],
                    rhs=a_sb[:, g, 1024 * h : 1024 * (h + 1)].bitcast(E2M1),
                    rhs_scale=a_sc[:, g, 512 * h : 512 * (h + 1)],
                    start=(g == 0),
                    stop=(g == G1 - 1),
                )

        def do_r(i, h):
            k = 2 * i + h
            if h == 0:
                r_bf[i] = work.tile([P, N], BF16, name="r_bf", bufs=5, align_bytes=64)
            cols = slice(512 * h, 512 * (h + 1))
            nc.vector.tensor_tensor(
                out=r_bf[i][:, cols].rearrange("p (u q e) -> p u q e", u=2, e=2),
                in0=acc1[k][:].rearrange("p (q u e) -> p u q e", u=2, e=2),
                in1=c_sb[i][:, cols].rearrange("p (q u e) -> p u q e", u=2, e=2),
                op=SUB,
            )

        def do_rt(i):
            r_t[i] = psum.tile([P, 512], F32, name="acc2")
            words = r_bf[i][:].bitcast(F32)
            for k in range(4):
                nc.tensor.transpose(r_t[i][:, k * P : (k + 1) * P], words[:, k * P : (k + 1) * P], ident[:])

        def do_rc(i):
            r_il[i] = work.tile([P, N], BF16, name="r_il", bufs=2, align_bytes=64)
            nc.scalar.copy(
                out=r_il[i][:].bitcast(F32).rearrange("p (h b u) -> p h b u", h=2, u=2),
                in_=r_t[i][:].rearrange("p (h u b) -> p h b u", h=2, u=2),
            )

        def do_qr(i):
            r_codes[i] = work.tile([P, G2 * P], U32, name="r_codes", bufs=4, align_bytes=64)
            r_sc[i] = work.tile([P, G2 * P], U8, name="r_sc", bufs=4, align_bytes=64)
            nc.vector.quantize_mx(out=r_codes[i][:].bitcast(E5M2), scales=r_sc[i][:], in_=r_il[i][:])

        def do_m2(i, n):
            acc2[i, n] = psum.tile([P, 512], F32, name="acc2")
            for h in range(G2):
                nc.tensor.matmul_mx(
                    out=acc2[i, n][:],
                    lhsT=r_codes[i][:, h * P : (h + 1) * P].bitcast(E5M2),
                    lhsT_scale=r_sc[i][:, h * P : (h + 1) * P],
                    rhs=k_codes[:, h, 512 * n : 512 * (n + 1)].bitcast(E4M3),
                    rhs_scale=k_sc[:, h, 512 * n : 512 * (n + 1)],
                    start=(h == 0),
                    stop=(h == G2 - 1),
                )

        def do_x(i):
            x06[i] = work.tile([P, N], F32, name="x06", bufs=3)
            nc.scalar.activation(out=x06[i][:], in_=x_sb[i][:], func=COPY, scale=-0.6)

        def do_o(i, n):
            cols = slice(512 * n, 512 * (n + 1))
            o = work.tile([P, 512], F32, name="o", bufs=5)
            nc.vector.scalar_tensor_tensor(
                out=o[:], in0=acc2[i, n][:], scalar=1.6, in1=x06[i][:, cols], op0=MULT, op1=ADD
            )
            nc.sync.dma_start(out=out[rows(i), cols], in_=o[:])

        def do_se(i):
            scaled[i] = work.tile([P, 512], F32, name="scaled", bufs=2)
            nc.scalar.activation(out=scaled[i][:], in_=acc2[i, 1][:], func=COPY, scale=1.6)

        def do_ga(i):
            o = work.tile([P, 512], F32, name="o", bufs=5)
            nc.gpsimd.tensor_tensor(out=o[:], in0=scaled[i][:], in1=x06[i][:, 512:1024], op=ADD)
            nc.sync.dma_start(out=out[rows(i), 512:1024], in_=o[:])

        def do_ik(h, n, part, eng):
            if part == 0:
                k_il[h, n] = work.tile([P, 512, 4], BF16, name="k_il", bufs=3, align_bytes=64)
            w0 = 256 * part
            src = k_raw[h][:, :, 512 * n + w0 : 512 * n + w0 + 256]
            dst = k_il[h, n][:, w0 : w0 + 256, :]
            if eng == "S":
                nc.scalar.copy(
                    out=dst.rearrange("p (c i) t -> p c t i", i=4), in_=src.rearrange("p t (c i) -> p c t i", i=4)
                )
            else:
                nc.gpsimd.tensor_scalar(
                    out=dst, in0=src.rearrange("p t w -> p w t"), scalar1=1.0, scalar2=0.0, op0=MULT, op1=ADD
                )

        def do_qk(h, n):
            cols = slice(512 * n, 512 * (n + 1))
            nc.vector.quantize_mx(
                out=k_codes[:, h, cols].bitcast(E4M3),
                scales=k_sc[:, h, cols],
                in_=k_il[h, n][:].rearrange("p w t -> p (w t)"),
            )

        actions = {
            "Tz": do_tz, "Ty": do_ty, "zr": do_zr, "v": do_v, "vm": do_vm, "gs": do_gs, "Tn": do_tn, "cp": do_cp,
            "qv": do_qv, "M1_": do_m1, "r": do_r, "rT": do_rt, "rc": do_rc, "qr": do_qr, "M2_": do_m2,
            "x06_": do_x, "o": do_o, "se": do_se, "ga": do_ga, "qk": do_qk,
        }
        for tok in ORDER.split():
            if tok.startswith("ik"):
                do_ik(int(tok[2]), int(tok[3]), int(tok[4]), tok[5])
                continue
            digits = "0123456789"
            name = tok
            args = []
            while name[len(name) - 1] in digits and not (name == "x06_"):
                args.append(int(name[len(name) - 1]))
                name = name[: len(name) - 1]
            actions[name](*reversed(args))
